import numpy as np
import ml_dtypes


def mxq(x, axis, fmt="e4m3"):
    dtype, down = {"e4m3": (ml_dtypes.float8_e4m3fn, 7), "e5m2": (ml_dtypes.float8_e5m2, 14)}[fmt]
    v = np.moveaxis(np.asarray(x, np.float32).astype(ml_dtypes.bfloat16).astype(np.float64), axis, -1)
    blocks = v.reshape(v.shape[:-1] + (-1, 32))
    amax = np.abs(blocks).max(-1, keepdims=True)
    byte = np.maximum(np.where(amax > 0, np.frexp(amax)[1] - 1 + 127, 0) - down, 1)
    scale = np.exp2(byte - 127.0)
    codes = (blocks / scale).astype(np.float32).astype(dtype).astype(np.float64)
    return np.moveaxis((codes * scale).reshape(v.shape), -1, axis)


WIDE = False


def mx_kscale(k):
    if not WIDE:
        return np.ones(k)
    levels = np.array([10, -10, 5, -5, 0])
    if k % 512:
        return np.exp2(np.random.permutation(np.resize(levels, k // 32))).repeat(32)
    a = np.empty((k // 512, 16))
    for p in range(k // 512):
        a[p, :8] = np.random.permutation(np.resize(levels, 8))
        for g in range(8):
            far = levels[np.abs(levels - a[p, g]) >= 10]
            a[p, g + 8] = far[np.random.randint(len(far))]
    return np.exp2(a.ravel()).repeat(32)


def f64(x):
    return np.asarray(x).astype(np.float64)


def striped(idx):
    return np.tile(np.asarray(idx).reshape(-1, 16).T, (8, 1)).astype(np.uint16)


def unstriped(offs):
    return offs[:16].T.reshape(-1).astype(np.int64)


E2M1 = np.array([0.0, 0.5, 1.0, 1.5, 2.0, 3.0, 4.0, 6.0, -0.0, -0.5, -1.0, -1.5, -2.0, -3.0, -4.0, -6.0])


def pack_weight(w, fmt):
    k, n = w.shape
    w = f64(np.asarray(w, np.float32).astype(ml_dtypes.bfloat16)).reshape(k // 32, 32, n)
    amax = np.abs(w).max(1)
    if fmt == "e4m3":
        byte = np.frexp(amax)[1] - 1 + 127 - 7
    else:
        mant, ex = np.frexp(amax / 6.0)
        byte = np.where(mant > 0.5, ex, ex - 1) + 127
    byte = np.clip(np.where(amax > 0, byte, 1), 1, 254)
    scaled = (w * np.exp2(127.0 - byte)[:, None, :]).reshape(k, n).astype(np.float32)
    by_word = np.ascontiguousarray(scaled.reshape(k // 512, 128, 4, n).transpose(0, 1, 3, 2))
    if fmt == "e4m3":
        words = by_word.astype(ml_dtypes.float8_e4m3fn).view(np.uint8)
    else:
        c = by_word.astype(ml_dtypes.float4_e2m1fn).view(np.uint8) & 0xF
        words = (c[..., 0::2] | (c[..., 1::2] << 4)).reshape(k // 512, 128, 2 * n)
    return np.ascontiguousarray(words), np.ascontiguousarray(byte.astype(np.uint8).reshape(k // 512, 16, n))


def unpack_weight(words, scales, fmt):
    g, _, n = scales.shape
    words = np.ascontiguousarray(words).reshape(g, 128, n, -1)
    if fmt == "e4m3":
        vals = words.view(ml_dtypes.float8_e4m3fn).astype(np.float64)
    else:
        nib = np.empty((g, 128, n, 4), np.uint8)
        nib[..., 0::2] = words & 0xF
        nib[..., 1::2] = words >> 4
        vals = E2M1[nib]
    vals = vals * np.repeat(np.exp2(scales.astype(np.float64) - 127.0), 8, axis=1)[..., None]
    return vals.transpose(0, 1, 3, 2).reshape(g * 512, n)


def sigmoid(v):
    return 1.0 / (1.0 + np.exp(-v))


def bf(x):
    return np.asarray(x, np.float32).astype(ml_dtypes.bfloat16)


def planes(Y):
    r, m = Y.shape
    b = f64(bf(Y)).reshape(r // 32, 32, m)
    amax = np.abs(b).max(1)
    byte = np.clip(np.where(amax > 0, np.frexp(amax)[1] - 1 + 127 - 7, 1), 1, 254)
    codes = (b * np.exp2(127.0 - byte)[:, None, :]).reshape(r, m).astype(np.float32).astype(ml_dtypes.float8_e4m3fn).view(np.uint8)
    words = codes.reshape(r // 512, 128, 4, m).transpose(0, 1, 3, 2)
    return np.ascontiguousarray(words), np.ascontiguousarray(byte.astype(np.uint8).reshape(r // 512, 16, m))


D, T, I, Q, E, U, M, C = 512, 2048, 512, 256, 512, 1024, 1024, 512


def setup_inputs():
    n = np.random.standard_normal
    idx = np.random.permutation(T)[:I]
    idx2 = np.random.permutation(U)[:I]
    idx3 = np.random.permutation(M)[:Q]
    fd = mx_kscale(D)
    fi = mx_kscale(I)
    fc = mx_kscale(C)
    ti = np.ones(T)
    ti[idx] = fi
    keysp = pack_weight(n((D, T)) / fd[:, None], "e2m1")
    return {
        "query": (n((D, Q)) * 0.7 / np.sqrt(D) * fd[:, None]).astype(np.float32),
        "query2": (n((D, Q)) * 0.7 / np.sqrt(D) * fd[:, None]).astype(np.float32),
        "keys_words": keysp[0],
        "keys_scales": keysp[1],
        "notes": (n((D, U)) / fd[:, None]).astype(np.float32),
        "os": (np.random.uniform(0.02, 0.08, (1, I)) * fi).astype(np.float32),
        "vals": (n((E, T)) / ti).astype(np.float32),
        "wm": (n((C, E)) * 1.0 / np.sqrt(C) * fc[:, None]).astype(np.float32),
        "mstore": (n((C, M)) / fc[:, None]).astype(np.float32),
        "offs": striped(idx),
        "offs2": striped(idx2),
        "offs3": striped(idx3),
    }


def reference(query, query2, keys_words, keys_scales, notes, os, vals, wm, mstore, offs, offs2, offs3):
    idx = unstriped(offs)
    idx2 = unstriped(offs2)
    idx3 = unstriped(offs3)
    keysu = unpack_weight(keys_words, keys_scales, "e2m1")
    queryq = mxq(f64(query), 0, "e4m3")
    keysidxg = keysu[:, idx]
    query2q = mxq(f64(query2), 0, "e4m3")
    notesidx2q = mxq(f64(notes)[:, idx2], 0, "e4m3")
    s = queryq.T @ keysidxg + query2q.T @ notesidx2q
    w = sigmoid(s)
    wo1 = w * f64(os)
    wt1 = wo1.T
    vt1 = f64(vals)[:, idx].T
    vt1q = mxq(vt1, 0, "e4m3")
    wt1q = mxq(wt1, 0, "e4m3")
    o = vt1q.T @ wt1q
    wmq = mxq(f64(wm), 0, "e4m3")
    mstoreq = mxq(f64(mstore), 0, "e4m3")
    me = wmq.T @ mstoreq
    y = o * me[:, idx3]
    words, scales = planes(y)
    return y, words, scales

@@ -1,0 +1,230 @@
+from contextlib import ExitStack
+
+import concourse.mybir as mybir
+from concourse.masks import make_identity
+
+D, T, I, Q, E, U, M, C = 512, 2048, 512, 256, 512, 1024, 1024, 512
+FLOPS = 2 * (2 * D * Q * I + I * E * Q + C * E * M)
+
+F32 = mybir.dt.float32
+BF16 = mybir.dt.bfloat16
+I32 = mybir.dt.int32
+U32 = mybir.dt.uint32
+U16 = mybir.dt.uint16
+U8 = mybir.dt.uint8
+FP8X4 = mybir.dt.float8_e4m3fn_x4
+FP4X4 = mybir.dt.float4_e2m1fn_x4
+COPY = mybir.ActivationFunctionType.Copy
+SIGMOID = mybir.ActivationFunctionType.Sigmoid
+MULT = mybir.AluOpType.mult
+
+P = 128
+PACK = 4
+BANK = 512
+
+
+def interleave(nc, dst, src):
+    nc.vector.tensor_copy(
+        out=dst.rearrange("p (c i) t -> p c t i", i=PACK),
+        in_=src.rearrange("p t (c i) -> p c t i", i=PACK),
+    )
+
+
+def deal_and_interleave(nc, dst, src):
+    nc.vector.tensor_copy(
+        out=dst.rearrange("p r s t -> p s t r"),
+        in_=src.rearrange("p t (s r) -> p s t r", r=PACK),
+    )
+
+
+def quantize(nc, pool, name, grouped, width):
+    codes = pool.tile([P, width], U32, name=name + "_codes", align_bytes=64)
+    scales = pool.tile([P, width], U8, name=name + "_scales", align_bytes=64)
+    nc.vector.quantize_mx(out=codes[:].bitcast(FP8X4), scales=scales[:], in_=grouped)
+    return codes, scales
+
+
+def tile_attend_twosources_remembered_lean_pl_kernel(
+    tc, query, query2, keys_words, keys_scales, notes, slot_factor, vals, wm, mstore, offs, offs2, offs3, out_0, out_1, out_2
+):
+    nc = tc.nc
+    with ExitStack() as ctx:
+        lists = ctx.enter_context(tc.tile_pool(name="lists", bufs=1))
+        sb = ctx.enter_context(tc.tile_pool(name="sb", bufs=1))
+        ps = ctx.enter_context(tc.psum_pool(name="ps", bufs=1))
+
+        key_scale_pool = sb.tile([P, T], U8, name="key_scale_pool", align_bytes=64)
+        nc.vector.memset(key_scale_pool[:].bitcast(I32), 0)
+
+        def load_rows(name, src):
+            t = sb.tile([P, PACK, src.shape[1]], F32, name=name)
+            nc.sync.dma_start(out=t[:], in_=src.rearrange("(p t) w -> p t w", t=PACK))
+            return t
+
+        def load_plane(name, src, t):
+            plane = sb.tile([P, src.shape[1]], F32, name=name)
+            nc.sync.dma_start(out=plane[:], in_=src.rearrange("(p t) w -> p t w", t=PACK)[:, t, :])
+            return plane
+
+        def load_list(name, src):
+            t = lists.tile([P, src.shape[1]], U16, name=name)
+            nc.sync.dma_start(t[:], src)
+            return t
+
+        idx = load_list("idx", offs)
+        key_word_pool = sb.tile([P, T], U16, name="key_word_pool", align_bytes=64)
+        nc.sync.dma_start(out=key_word_pool[:].bitcast(I32), in_=keys_words[0].bitcast(I32))
+        for quad in range(4):
+            nc.sync.dma_start(
+                out=key_scale_pool[32 * quad : 32 * quad + 4, :].bitcast(I32),
+                in_=keys_scales[0, 4 * quad : 4 * quad + 4, :].bitcast(I32),
+            )
+        wm_raw = load_rows("wm_raw", wm)
+        idx2 = load_list("idx2", offs2)
+        note_pool0 = load_plane("note_pool0", notes, 0)
+        ms_raw0 = load_rows("ms_raw0", mstore[:, 0:BANK])
+        note_pool1 = load_plane("note_pool1", notes, 1)
+        q_raw0 = load_rows("q_raw0", query)
+        ms_raw1 = load_rows("ms_raw1", mstore[:, BANK:M])
+        idx3 = load_list("idx3", offs3)
+        note_pool2 = load_plane("note_pool2", notes, 2)
+        note_pool3 = load_plane("note_pool3", notes, 3)
+        q_raw1 = load_rows("q_raw1", query2)
+        os_sb = sb.tile([P, PACK], F32, name="os_sb")
+        nc.sync.dma_start(out=os_sb[:], in_=slot_factor.rearrange("o (p r) -> (o p) r", r=PACK))
+        val_pool0 = load_plane("val_pool0", vals, 0)
+        val_pool1 = load_plane("val_pool1", vals, 1)
+        val_pool2 = load_plane("val_pool2", vals, 2)
+        val_pool3 = load_plane("val_pool3", vals, 3)
+
+        ident = sb.tile([P, P], F32, name="ident")
+        make_identity(nc, ident[:])
+        me = [sb.tile([P, M], F32, name="me%d" % j) for j in range(PACK)]
+        note_listed = sb.tile([P, PACK, I], BF16, name="note_listed", align_bytes=64)
+        me_listed = sb.tile([P, PACK, Q], F32, name="me_listed")
+        y = sb.tile([P, PACK, Q], F32, name="y")
+        out_rows = out_0.rearrange("(p j) q -> p j q", j=PACK)
+        key_scales = sb.tile([P, I], U8, name="key_scales", align_bytes=64)
+        nc.vector.tensor_copy(out=key_scales[:].rearrange("p (r s) -> p s r", r=PACK), in_=key_scale_pool[:].indirect(idx[:]))
+        key_listed = sb.tile([P, I], U16, name="key_listed", align_bytes=64)
+        nc.vector.tensor_copy(out=key_listed[:], in_=key_word_pool[:].indirect(idx[:]))
+        key_words = sb.tile([P, I], U16, name="key_words", align_bytes=64)
+        nc.vector.tensor_copy(out=key_words[:].rearrange("p (r s) -> p r s", r=PACK), in_=key_listed[:].rearrange("p (s r) -> p r s", r=PACK))
+        wm_bf = sb.tile([P, PACK, P, PACK], BF16, name="wm_bf", align_bytes=64)
+        deal_and_interleave(nc, wm_bf[:], wm_raw[:])
+        wm_codes, wm_scales = quantize(nc, sb, "wm", wm_bf[:].rearrange("p r s t -> p (r s t)"), E)
+        nc.scalar.activation(note_listed[:, 0, :], note_pool0[:].indirect(idx2[:]), COPY)
+        ms_bf0 = sb.tile([P, BANK, PACK], BF16, name="ms_bf0", align_bytes=64)
+        interleave(nc, ms_bf0[:], ms_raw0[:])
+        ms0_codes, ms0_scales = quantize(nc, sb, "ms0", ms_bf0[:].rearrange("p w t -> p (w t)"), BANK)
+        acc = ps.tile([P, BANK], F32, name="me_acc", tag="bank0")
+        nc.tensor.matmul_mx(out=acc[:], lhsT=wm_codes[:, 0:128].bitcast(FP8X4), lhsT_scale=wm_scales[:, 0:128], rhs=ms0_codes[:, 0:BANK].bitcast(FP8X4), rhs_scale=ms0_scales[:, 0:BANK], start=True, stop=True)
+        nc.scalar.copy(out=me[0][:, 0 * BANK : 1 * BANK], in_=acc[:])
+        acc = ps.tile([P, BANK], F32, name="me_acc", tag="bank1")
+        nc.tensor.matmul_mx(out=acc[:], lhsT=wm_codes[:, 128:256].bitcast(FP8X4), lhsT_scale=wm_scales[:, 128:256], rhs=ms0_codes[:, 0:BANK].bitcast(FP8X4), rhs_scale=ms0_scales[:, 0:BANK], start=True, stop=True)
+        nc.scalar.copy(out=me[1][:, 0 * BANK : 1 * BANK], in_=acc[:])
+        acc = ps.tile([P, BANK], F32, name="me_acc", tag="bank2")
+        nc.tensor.matmul_mx(out=acc[:], lhsT=wm_codes[:, 256:384].bitcast(FP8X4), lhsT_scale=wm_scales[:, 256:384], rhs=ms0_codes[:, 0:BANK].bitcast(FP8X4), rhs_scale=ms0_scales[:, 0:BANK], start=True, stop=True)
+        nc.scalar.copy(out=me[2][:, 0 * BANK : 1 * BANK], in_=acc[:])
+        acc = ps.tile([P, BANK], F32, name="me_acc", tag="bank3")
+        nc.tensor.matmul_mx(out=acc[:], lhsT=wm_codes[:, 384:512].bitcast(FP8X4), lhsT_scale=wm_scales[:, 384:512], rhs=ms0_codes[:, 0:BANK].bitcast(FP8X4), rhs_scale=ms0_scales[:, 0:BANK], start=True, stop=True)
+        nc.scalar.copy(out=me[3][:, 0 * BANK : 1 * BANK], in_=acc[:])
+        nc.scalar.activation(note_listed[:, 1, :], note_pool1[:].indirect(idx2[:]), COPY)
+        q0_bf = sb.tile([P, Q, PACK], BF16, name="q0_bf", align_bytes=64)
+        interleave(nc, q0_bf[:], q_raw0[:])
+        q0_codes, q0_scales = quantize(nc, sb, "q0", q0_bf[:].rearrange("p w t -> p (w t)"), Q)
+        scores = [ps.tile([P, PACK, P], F32, name="scores%d" % h, tag="bank%d" % (4 + h)) for h in range(2)]
+        for h in range(2):
+            for r in range(PACK):
+                nc.tensor.matmul_mx(out=scores[h][:, r, :], lhsT=key_words[:, r * P : (r + 1) * P].bitcast(FP4X4), lhsT_scale=key_scales[:, r * P : (r + 1) * P], rhs=q0_codes[:, h * P : (h + 1) * P].bitcast(FP8X4), rhs_scale=q0_scales[:, h * P : (h + 1) * P], start=r == 0, stop=False)
+        ms_bf1 = sb.tile([P, BANK, PACK], BF16, name="ms_bf1", align_bytes=64)
+        interleave(nc, ms_bf1[:], ms_raw1[:])
+        ms1_codes, ms1_scales = quantize(nc, sb, "ms1", ms_bf1[:].rearrange("p w t -> p (w t)"), BANK)
+        nc.scalar.activation(note_listed[:, 2, :], note_pool2[:].indirect(idx2[:]), COPY)
+        nc.scalar.activation(note_listed[:, 3, :], note_pool3[:].indirect(idx2[:]), COPY)
+        note_bf = sb.tile([P, PACK, P, PACK], BF16, name="note_bf", align_bytes=64)
+        deal_and_interleave(nc, note_bf[:], note_listed[:])
+        note_codes, note_scales = quantize(nc, sb, "note", note_bf[:].rearrange("p r s t -> p (r s t)"), I)
+        q1_bf = sb.tile([P, Q, PACK], BF16, name="q1_bf", align_bytes=64)
+        interleave(nc, q1_bf[:], q_raw1[:])
+        q1_codes, q1_scales = quantize(nc, sb, "q1", q1_bf[:].rearrange("p w t -> p (w t)"), Q)
+        w_bf = sb.tile([P, Q, PACK], BF16, name="w_bf", align_bytes=64)
+        for h in range(2):
+            for r in range(PACK):
+                nc.tensor.matmul_mx(out=scores[h][:, r, :], lhsT=note_codes[:, r * P : (r + 1) * P].bitcast(FP8X4), lhsT_scale=note_scales[:, r * P : (r + 1) * P], rhs=q1_codes[:, h * P : (h + 1) * P].bitcast(FP8X4), rhs_scale=q1_scales[:, h * P : (h + 1) * P], start=False, stop=r == PACK - 1)
+            gate = sb.tile([P, P, PACK], F32, name="gate%d" % h)
+            nc.scalar.activation(gate[:], scores[h][:].rearrange("p r q -> p q r"), SIGMOID)
+            nc.vector.tensor_tensor(out=w_bf[:, h * P : (h + 1) * P, :], in0=gate[:], in1=os_sb[:].unsqueeze(1).to_broadcast([P, P, PACK]), op=MULT)
+        w_codes, w_scales = quantize(nc, sb, "w", w_bf[:].rearrange("p q r -> p (q r)"), Q)
+        acc = ps.tile([P, BANK], F32, name="me_acc", tag="bank6")
+        nc.tensor.matmul_mx(out=acc[:], lhsT=wm_codes[:, 0:128].bitcast(FP8X4), lhsT_scale=wm_scales[:, 0:128], rhs=ms1_codes[:, 0:BANK].bitcast(FP8X4), rhs_scale=ms1_scales[:, 0:BANK], start=True, stop=True)
+        nc.scalar.copy(out=me[0][:, 1 * BANK : 2 * BANK], in_=acc[:])
+        acc = ps.tile([P, BANK], F32, name="me_acc", tag="bank7")
+        nc.tensor.matmul_mx(out=acc[:], lhsT=wm_codes[:, 128:256].bitcast(FP8X4), lhsT_scale=wm_scales[:, 128:256], rhs=ms1_codes[:, 0:BANK].bitcast(FP8X4), rhs_scale=ms1_scales[:, 0:BANK], start=True, stop=True)
+        nc.scalar.copy(out=me[1][:, 1 * BANK : 2 * BANK], in_=acc[:])
+        acc = ps.tile([P, BANK], F32, name="me_acc", tag="bank0")
+        nc.tensor.matmul_mx(out=acc[:], lhsT=wm_codes[:, 256:384].bitcast(FP8X4), lhsT_scale=wm_scales[:, 256:384], rhs=ms1_codes[:, 0:BANK].bitcast(FP8X4), rhs_scale=ms1_scales[:, 0:BANK], start=True, stop=True)
+        nc.scalar.copy(out=me[2][:, 1 * BANK : 2 * BANK], in_=acc[:])
+        acc = ps.tile([P, BANK], F32, name="me_acc", tag="bank1")
+        nc.tensor.matmul_mx(out=acc[:], lhsT=wm_codes[:, 384:512].bitcast(FP8X4), lhsT_scale=wm_scales[:, 384:512], rhs=ms1_codes[:, 0:BANK].bitcast(FP8X4), rhs_scale=ms1_scales[:, 0:BANK], start=True, stop=True)
+        nc.scalar.copy(out=me[3][:, 1 * BANK : 2 * BANK], in_=acc[:])
+        nc.vector.tensor_copy(out=me_listed[:, 0, :], in_=me[0][:].indirect(idx3[:]))
+        nc.scalar.activation(me_listed[:, 1, :], me[1][:].indirect(idx3[:]), COPY)
+        nc.scalar.activation(me_listed[:, 2, :], me[2][:].indirect(idx3[:]), COPY)
+        nc.scalar.activation(me_listed[:, 3, :], me[3][:].indirect(idx3[:]), COPY)
+        listed = sb.tile([P, I], BF16, name="val_listed0", align_bytes=64)
+        nc.vector.tensor_copy(out=listed[:], in_=val_pool0[:].indirect(idx[:]))
+        pairs = listed[:].bitcast(F32)
+        turned = ps.tile([P, 2, P], F32, name="turned", tag="bank4")
+        for u in range(2):
+            nc.tensor.transpose(turned[:, u, :], pairs[:, u::2], ident[:])
+        val_bf = sb.tile([P, P, PACK], BF16, name="val_bf0", align_bytes=64)
+        nc.vector.tensor_copy(out=val_bf[:].bitcast(F32), in_=turned[:].rearrange("p u e -> p e u"))
+        val0_codes, val0_scales = quantize(nc, sb, "val0", val_bf[:].rearrange("p e r -> p (e r)"), P)
+        listed = sb.tile([P, I], BF16, name="val_listed1", align_bytes=64)
+        nc.scalar.activation(listed[:], val_pool1[:].indirect(idx[:]), COPY)
+        pairs = listed[:].bitcast(F32)
+        turned = ps.tile([P, 2, P], F32, name="turned", tag="bank5")
+        for u in range(2):
+            nc.tensor.transpose(turned[:, u, :], pairs[:, u::2], ident[:])
+        val_bf = sb.tile([P, P, PACK], BF16, name="val_bf1", align_bytes=64)
+        nc.vector.tensor_copy(out=val_bf[:].bitcast(F32), in_=turned[:].rearrange("p u e -> p e u"))
+        val1_codes, val1_scales = quantize(nc, sb, "val1", val_bf[:].rearrange("p e r -> p (e r)"), P)
+        listed = sb.tile([P, I], BF16, name="val_listed2", align_bytes=64)
+        nc.scalar.activation(listed[:], val_pool2[:].indirect(idx[:]), COPY)
+        pairs = listed[:].bitcast(F32)
+        turned = ps.tile([P, 2, P], F32, name="turned", tag="bank6")
+        for u in range(2):
+            nc.tensor.transpose(turned[:, u, :], pairs[:, u::2], ident[:])
+        val_bf = sb.tile([P, P, PACK], BF16, name="val_bf2", align_bytes=64)
+        nc.vector.tensor_copy(out=val_bf[:].bitcast(F32), in_=turned[:].rearrange("p u e -> p e u"))
+        val2_codes, val2_scales = quantize(nc, sb, "val2", val_bf[:].rearrange("p e r -> p (e r)"), P)
+        listed = sb.tile([P, I], BF16, name="val_listed3", align_bytes=64)
+        nc.scalar.activation(listed[:], val_pool3[:].indirect(idx[:]), COPY)
+        pairs = listed[:].bitcast(F32)
+        turned = ps.tile([P, 2, P], F32, name="turned", tag="bank7")
+        for u in range(2):
+            nc.tensor.transpose(turned[:, u, :], pairs[:, u::2], ident[:])
+        val_bf = sb.tile([P, P, PACK], BF16, name="val_bf3", align_bytes=64)
+        nc.scalar.copy(out=val_bf[:].bitcast(F32), in_=turned[:].rearrange("p u e -> p e u"))
+        val3_codes, val3_scales = quantize(nc, sb, "val3", val_bf[:].rearrange("p e r -> p (e r)"), P)
+        o01 = ps.tile([P, 2, Q], F32, name="o01", tag="bank6")
+        nc.tensor.matmul_mx(out=o01[:, 0, :], lhsT=val0_codes[:, 0:P].bitcast(FP8X4), lhsT_scale=val0_scales[:, 0:P], rhs=w_codes[:, 0:Q].bitcast(FP8X4), rhs_scale=w_scales[:, 0:Q], start=True, stop=True)
+        nc.tensor.matmul_mx(out=o01[:, 1, :], lhsT=val1_codes[:, 0:P].bitcast(FP8X4), lhsT_scale=val1_scales[:, 0:P], rhs=w_codes[:, 0:Q].bitcast(FP8X4), rhs_scale=w_scales[:, 0:Q], start=True, stop=True)
+        nc.vector.tensor_tensor(out=y[:, 0:2, :], in0=o01[:], in1=me_listed[:, 0:2, :], op=MULT)
+        nc.sync.dma_start(out=out_rows[:, 0:2, :], in_=y[:, 0:2, :])
+        o = ps.tile([P, Q], F32, name="o", tag="bank4")
+        nc.tensor.matmul_mx(out=o[:], lhsT=val2_codes[:, 0:P].bitcast(FP8X4), lhsT_scale=val2_scales[:, 0:P], rhs=w_codes[:, 0:Q].bitcast(FP8X4), rhs_scale=w_scales[:, 0:Q], start=True, stop=True)
+        nc.vector.tensor_tensor(out=y[:, 2, :], in0=o[:], in1=me_listed[:, 2, :], op=MULT)
+        nc.sync.dma_start(out=out_rows[:, 2, :], in_=y[:, 2, :])
+        o = ps.tile([P, Q], F32, name="o", tag="bank0")
+        nc.tensor.matmul_mx(out=o[:], lhsT=val3_codes[:, 0:P].bitcast(FP8X4), lhsT_scale=val3_scales[:, 0:P], rhs=w_codes[:, 0:Q].bitcast(FP8X4), rhs_scale=w_scales[:, 0:Q], start=True, stop=True)
+        nc.vector.tensor_tensor(out=y[:, 3, :], in0=o[:], in1=me_listed[:, 3, :], op=MULT)
+        nc.sync.dma_start(out=out_rows[:, 3, :], in_=y[:, 3, :])
+        y_bf = sb.tile([P, Q, PACK], BF16, name="y_bf", align_bytes=64)
+        interleave(nc, y_bf[:], y[:])
+        y_codes, y_scales = quantize(nc, sb, "y", y_bf[:].rearrange("p q j -> p (q j)"), Q)
+        nc.sync.dma_start(out=out_1[0].rearrange("p q j -> p (q j)").bitcast(I32), in_=y_codes[:].bitcast(I32))
+        for quad in range(4):
+            queue = nc.scalar if quad % 2 == 0 else nc.sync
+            queue.dma_start(out=out_2[0, 4 * quad : 4 * quad + 4, :].bitcast(I32), in_=y_scales[32 * quad : 32 * quad + 4, :].bitcast(I32))

@@ -104,6 +104,8 @@ def tile_attend_twosources_remembered_lean_pl_kernel(
         me_listed = sb.tile([P, PACK, Q], F32, name="me_listed")
         y = sb.tile([P, PACK, Q], F32, name="y")
         out_rows = out_0.rearrange("(p j) q -> p j q", j=PACK)
+        warm = sb.tile([P, 1], F32, name="warm")
+        nc.scalar.activation(warm[:], ident[:, 0:1], SIGMOID)
         key_scales = sb.tile([P, I], U8, name="key_scales", align_bytes=64)
         nc.vector.tensor_copy(out=key_scales[:].rearrange("p (r s) -> p s r", r=PACK), in_=key_scale_pool[:].indirect(idx[:]))
         key_listed = sb.tile([P, I], U16, name="key_listed", align_bytes=64)

@@ -21,10 +21,13 @@ MULT = mybir.AluOpType.mult
 P = 128
 PACK = 4
 BANK = 512
+ALIGN = 64
+LIST_COLS = I // 16
+Y_VECTOR_COLS = 160
 
 
-def interleave(nc, dst, src):
-    nc.vector.tensor_copy(
+def interleave(copy, dst, src):
+    copy(
         out=dst.rearrange("p (c i) t -> p c t i", i=PACK),
         in_=src.rearrange("p t (c i) -> p c t i", i=PACK),
     )
@@ -37,11 +40,28 @@ def deal_and_interleave(nc, dst, src):
     )
 
 
-def quantize(nc, pool, name, grouped, width):
-    codes = pool.tile([P, width], U32, name=name + "_codes", align_bytes=64)
-    scales = pool.tile([P, width], U8, name=name + "_scales", align_bytes=64)
+def quantize(nc, pool, name, grouped):
+    width = grouped.shape[1] // PACK
+    codes = pool.tile([P, width], U32, name=name + "_codes", align_bytes=ALIGN)
+    scales = pool.tile([P, width], U8, name=name + "_scales", align_bytes=ALIGN)
     nc.vector.quantize_mx(out=codes[:].bitcast(FP8X4), scales=scales[:], in_=grouped)
     return codes, scales
+
+
+def product(nc, out, stationary, s_cols, moving, m_cols, start=True, stop=True, s_dtype=FP8X4):
+    nc.tensor.matmul_mx(
+        out=out,
+        lhsT=stationary[0][:, s_cols].bitcast(s_dtype),
+        lhsT_scale=stationary[1][:, s_cols],
+        rhs=moving[0][:, m_cols].bitcast(FP8X4),
+        rhs_scale=moving[1][:, m_cols],
+        start=start,
+        stop=stop,
+    )
+
+
+def block(k, width=P):
+    return slice(k * width, (k + 1) * width)
 
 
 def tile_attend_twosources_remembered_lean_pl_kernel(
@@ -51,182 +71,185 @@ def tile_attend_twosources_remembered_lean_pl_kernel(
     with ExitStack() as ctx:
         lists = ctx.enter_context(tc.tile_pool(name="lists", bufs=1))
         sb = ctx.enter_context(tc.tile_pool(name="sb", bufs=1))
+        reused = ctx.enter_context(tc.tile_pool(name="reused", bufs=1))
         ps = ctx.enter_context(tc.psum_pool(name="ps", bufs=1))
 
-        key_scale_pool = sb.tile([P, T], U8, name="key_scale_pool", align_bytes=64)
-        nc.vector.memset(key_scale_pool[:].bitcast(I32), 0)
+        def bank_tile(name, shape, bank):
+            return ps.tile(shape, F32, name=name, tag="bank%d" % bank)
 
         def load_rows(name, src):
-            t = sb.tile([P, PACK, src.shape[1]], F32, name=name)
-            nc.sync.dma_start(out=t[:], in_=src.rearrange("(p t) w -> p t w", t=PACK))
-            return t
+            rows = sb.tile([P, PACK, src.shape[1]], F32, name=name)
+            nc.sync.dma_start(out=rows[:], in_=src.rearrange("(p t) w -> p t w", t=PACK))
+            return rows
 
-        def load_plane(name, src, t):
-            plane = sb.tile([P, src.shape[1]], F32, name=name)
+        def load_plane(name, src, t, pool=sb, offset=None):
+            plane = pool.tile([P, src.shape[1]], F32, name=name, align_bytes=ALIGN, offset=offset)
             nc.sync.dma_start(out=plane[:], in_=src.rearrange("(p t) w -> p t w", t=PACK)[:, t, :])
             return plane
 
         def load_list(name, src):
-            t = lists.tile([P, src.shape[1]], U16, name=name)
-            nc.sync.dma_start(t[:], src)
-            return t
+            offsets = lists.tile([P, src.shape[1]], U16, name=name)
+            nc.sync.dma_start(offsets[:], src)
+            return offsets
 
-        idx = load_list("idx", offs)
-        key_word_pool = sb.tile([P, T], U16, name="key_word_pool", align_bytes=64)
+        def gather_vector(out, window, offsets):
+            nc.vector.tensor_copy(out=out, in_=window[:].indirect(offsets))
+
+        def gather_scalar(out, window, offsets):
+            nc.scalar.activation(out, window[:].indirect(offsets), COPY)
+
+        warm_in = sb.tile([P, 1], F32, name="warm_in")
+        nc.vector.memset(warm_in[:], 0.0)
+        warm_out = sb.tile([P, 1], F32, name="warm_out")
+        nc.scalar.activation(warm_out[:], warm_in[:], SIGMOID)
+
+        key_scale_pool = sb.tile([P, T], U8, name="key_scale_pool", align_bytes=ALIGN)
+        nc.vector.memset(key_scale_pool[:].bitcast(I32), 0)
+
+        key_word_pool = sb.tile([P, T], U16, name="key_word_pool", align_bytes=ALIGN)
         nc.sync.dma_start(out=key_word_pool[:].bitcast(I32), in_=keys_words[0].bitcast(I32))
+        idx = load_list("idx", offs)
+        wm_raw = load_rows("wm_raw", wm)
+        idx2 = load_list("idx2", offs2)
+        note_pool = [load_plane("note_pool0", notes, 0)]
+        ms_raw = [load_rows("ms_raw0", mstore[:, block(0, BANK)])]
+        note_pool.append(load_plane("note_pool1", notes, 1))
         for quad in range(4):
             nc.sync.dma_start(
                 out=key_scale_pool[32 * quad : 32 * quad + 4, :].bitcast(I32),
                 in_=keys_scales[0, 4 * quad : 4 * quad + 4, :].bitcast(I32),
             )
-        wm_raw = load_rows("wm_raw", wm)
-        idx2 = load_list("idx2", offs2)
-        note_pool0 = load_plane("note_pool0", notes, 0)
-        ms_raw0 = load_rows("ms_raw0", mstore[:, 0:BANK])
-        note_pool1 = load_plane("note_pool1", notes, 1)
-        q_raw0 = load_rows("q_raw0", query)
-        ms_raw1 = load_rows("ms_raw1", mstore[:, BANK:M])
+        ms_raw.append(load_rows("ms_raw1", mstore[:, block(1, BANK)]))
+        note_pool.append(load_plane("note_pool2", notes, 2))
+        note_pool.append(load_plane("note_pool3", notes, 3))
         idx3 = load_list("idx3", offs3)
-        note_pool2 = load_plane("note_pool2", notes, 2)
-        note_pool3 = load_plane("note_pool3", notes, 3)
-        q_raw1 = load_rows("q_raw1", query2)
+        q2_raw = load_rows("q2_raw", query2)
+        q_raw = load_rows("q_raw", query)
         os_sb = sb.tile([P, PACK], F32, name="os_sb")
         nc.sync.dma_start(out=os_sb[:], in_=slot_factor.rearrange("o (p r) -> (o p) r", r=PACK))
-        val_pool0 = load_plane("val_pool0", vals, 0)
-        val_pool1 = load_plane("val_pool1", vals, 1)
-        val_pool2 = load_plane("val_pool2", vals, 2)
-        val_pool3 = load_plane("val_pool3", vals, 3)
+        val_pool = [load_plane("val_pool%d" % j, vals, j) for j in range(PACK - 1)]
+        val_pool.append(load_plane("val_pool3", vals, 3, reused, 0))
 
         ident = sb.tile([P, P], F32, name="ident")
         make_identity(nc, ident[:])
+
         me = [sb.tile([P, M], F32, name="me%d" % j) for j in range(PACK)]
-        note_listed = sb.tile([P, PACK, I], BF16, name="note_listed", align_bytes=64)
-        me_listed = sb.tile([P, PACK, Q], F32, name="me_listed")
-        y = sb.tile([P, PACK, Q], F32, name="y")
-        out_rows = out_0.rearrange("(p j) q -> p j q", j=PACK)
-        warm = sb.tile([P, 1], F32, name="warm")
-        nc.scalar.activation(warm[:], ident[:, 0:1], SIGMOID)
-        key_scales = sb.tile([P, I], U8, name="key_scales", align_bytes=64)
-        nc.vector.tensor_copy(out=key_scales[:].rearrange("p (r s) -> p s r", r=PACK), in_=key_scale_pool[:].indirect(idx[:]))
-        key_listed = sb.tile([P, I], U16, name="key_listed", align_bytes=64)
-        nc.vector.tensor_copy(out=key_listed[:], in_=key_word_pool[:].indirect(idx[:]))
-        key_words = sb.tile([P, I], U16, name="key_words", align_bytes=64)
-        nc.vector.tensor_copy(out=key_words[:].rearrange("p (r s) -> p r s", r=PACK), in_=key_listed[:].rearrange("p (s r) -> p r s", r=PACK))
-        wm_bf = sb.tile([P, PACK, P, PACK], BF16, name="wm_bf", align_bytes=64)
+        note_listed = sb.tile([P, PACK, I], BF16, name="note_listed", align_bytes=ALIGN)
+
+        key_listed = sb.tile([P, I], U16, name="key_listed", align_bytes=ALIGN)
+        gather_vector(key_listed[:], key_word_pool, idx[:])
+        key_words = sb.tile([P, I], U16, name="key_words", align_bytes=ALIGN)
+        nc.vector.tensor_copy(
+            out=key_words[:].rearrange("p (r s) -> p r s", r=PACK), in_=key_listed[:].rearrange("p (s r) -> p r s", r=PACK)
+        )
+
+        wm_bf = sb.tile([P, PACK, P, PACK], BF16, name="wm_bf", align_bytes=ALIGN)
         deal_and_interleave(nc, wm_bf[:], wm_raw[:])
-        wm_codes, wm_scales = quantize(nc, sb, "wm", wm_bf[:].rearrange("p r s t -> p (r s t)"), E)
-        nc.scalar.activation(note_listed[:, 0, :], note_pool0[:].indirect(idx2[:]), COPY)
-        ms_bf0 = sb.tile([P, BANK, PACK], BF16, name="ms_bf0", align_bytes=64)
-        interleave(nc, ms_bf0[:], ms_raw0[:])
-        ms0_codes, ms0_scales = quantize(nc, sb, "ms0", ms_bf0[:].rearrange("p w t -> p (w t)"), BANK)
-        acc = ps.tile([P, BANK], F32, name="me_acc", tag="bank0")
-        nc.tensor.matmul_mx(out=acc[:], lhsT=wm_codes[:, 0:128].bitcast(FP8X4), lhsT_scale=wm_scales[:, 0:128], rhs=ms0_codes[:, 0:BANK].bitcast(FP8X4), rhs_scale=ms0_scales[:, 0:BANK], start=True, stop=True)
-        nc.scalar.copy(out=me[0][:, 0 * BANK : 1 * BANK], in_=acc[:])
-        acc = ps.tile([P, BANK], F32, name="me_acc", tag="bank1")
-        nc.tensor.matmul_mx(out=acc[:], lhsT=wm_codes[:, 128:256].bitcast(FP8X4), lhsT_scale=wm_scales[:, 128:256], rhs=ms0_codes[:, 0:BANK].bitcast(FP8X4), rhs_scale=ms0_scales[:, 0:BANK], start=True, stop=True)
-        nc.scalar.copy(out=me[1][:, 0 * BANK : 1 * BANK], in_=acc[:])
-        acc = ps.tile([P, BANK], F32, name="me_acc", tag="bank2")
-        nc.tensor.matmul_mx(out=acc[:], lhsT=wm_codes[:, 256:384].bitcast(FP8X4), lhsT_scale=wm_scales[:, 256:384], rhs=ms0_codes[:, 0:BANK].bitcast(FP8X4), rhs_scale=ms0_scales[:, 0:BANK], start=True, stop=True)
-        nc.scalar.copy(out=me[2][:, 0 * BANK : 1 * BANK], in_=acc[:])
-        acc = ps.tile([P, BANK], F32, name="me_acc", tag="bank3")
-        nc.tensor.matmul_mx(out=acc[:], lhsT=wm_codes[:, 384:512].bitcast(FP8X4), lhsT_scale=wm_scales[:, 384:512], rhs=ms0_codes[:, 0:BANK].bitcast(FP8X4), rhs_scale=ms0_scales[:, 0:BANK], start=True, stop=True)
-        nc.scalar.copy(out=me[3][:, 0 * BANK : 1 * BANK], in_=acc[:])
-        nc.scalar.activation(note_listed[:, 1, :], note_pool1[:].indirect(idx2[:]), COPY)
-        q0_bf = sb.tile([P, Q, PACK], BF16, name="q0_bf", align_bytes=64)
-        interleave(nc, q0_bf[:], q_raw0[:])
-        q0_codes, q0_scales = quantize(nc, sb, "q0", q0_bf[:].rearrange("p w t -> p (w t)"), Q)
-        scores = [ps.tile([P, PACK, P], F32, name="scores%d" % h, tag="bank%d" % (4 + h)) for h in range(2)]
-        for h in range(2):
-            for r in range(PACK):
-                nc.tensor.matmul_mx(out=scores[h][:, r, :], lhsT=key_words[:, r * P : (r + 1) * P].bitcast(FP4X4), lhsT_scale=key_scales[:, r * P : (r + 1) * P], rhs=q0_codes[:, h * P : (h + 1) * P].bitcast(FP8X4), rhs_scale=q0_scales[:, h * P : (h + 1) * P], start=r == 0, stop=False)
-        ms_bf1 = sb.tile([P, BANK, PACK], BF16, name="ms_bf1", align_bytes=64)
-        interleave(nc, ms_bf1[:], ms_raw1[:])
-        ms1_codes, ms1_scales = quantize(nc, sb, "ms1", ms_bf1[:].rearrange("p w t -> p (w t)"), BANK)
-        nc.scalar.activation(note_listed[:, 2, :], note_pool2[:].indirect(idx2[:]), COPY)
-        nc.scalar.activation(note_listed[:, 3, :], note_pool3[:].indirect(idx2[:]), COPY)
-        note_bf = sb.tile([P, PACK, P, PACK], BF16, name="note_bf", align_bytes=64)
+        wm_mx = quantize(nc, sb, "wm", wm_bf[:].rearrange("p r s t -> p (r s t)"))
+
+        def quantize_store_half(h):
+            ms_bf = sb.tile([P, BANK, PACK], BF16, name="ms_bf%d" % h, align_bytes=ALIGN)
+            interleave(nc.vector.tensor_copy, ms_bf[:], ms_raw[h][:])
+            return quantize(nc, sb, "ms%d" % h, ms_bf[:].rearrange("p w t -> p (w t)"))
+
+        def make_memories(h, ms_mx):
+            for j in range(PACK):
+                acc = bank_tile("me_acc", [P, BANK], PACK * h + j)
+                product(nc, acc[:], wm_mx, block(j), ms_mx, block(0, BANK))
+                nc.scalar.copy(out=me[j][:, block(h, BANK)], in_=acc[:])
+
+        gather_scalar(note_listed[:, 0, :], note_pool[0], idx2[:])
+        make_memories(0, quantize_store_half(0))
+        gather_scalar(note_listed[:, 1, :], note_pool[1], idx2[:])
+        key_scales = sb.tile([P, I], U8, name="key_scales", align_bytes=ALIGN)
+        gather_vector(key_scales[:].rearrange("p (r s) -> p s r", r=PACK), key_scale_pool, idx[:])
+        ms1_mx = quantize_store_half(1)
+        gather_scalar(note_listed[:, 2, :], note_pool[2], idx2[:])
+        make_memories(1, ms1_mx)
+        gather_vector(note_listed[:, 3, :], note_pool[3], idx2[:])
+
+        note_bf = sb.tile([P, PACK, P, PACK], BF16, name="note_bf", align_bytes=ALIGN)
         deal_and_interleave(nc, note_bf[:], note_listed[:])
-        note_codes, note_scales = quantize(nc, sb, "note", note_bf[:].rearrange("p r s t -> p (r s t)"), I)
-        q1_bf = sb.tile([P, Q, PACK], BF16, name="q1_bf", align_bytes=64)
-        interleave(nc, q1_bf[:], q_raw1[:])
-        q1_codes, q1_scales = quantize(nc, sb, "q1", q1_bf[:].rearrange("p w t -> p (w t)"), Q)
-        w_bf = sb.tile([P, Q, PACK], BF16, name="w_bf", align_bytes=64)
+        q2_bf = sb.tile([P, Q, PACK], BF16, name="q2_bf", align_bytes=ALIGN)
+        interleave(nc.vector.tensor_copy, q2_bf[:], q2_raw[:])
+        note_mx = quantize(nc, sb, "note", note_bf[:].rearrange("p r s t -> p (r s t)"))
+        q2_mx = quantize(nc, sb, "q2", q2_bf[:].rearrange("p w t -> p (w t)"))
+        scores = [bank_tile("scores%d" % h, [P, PACK, P], h) for h in range(2)]
         for h in range(2):
             for r in range(PACK):
-                nc.tensor.matmul_mx(out=scores[h][:, r, :], lhsT=note_codes[:, r * P : (r + 1) * P].bitcast(FP8X4), lhsT_scale=note_scales[:, r * P : (r + 1) * P], rhs=q1_codes[:, h * P : (h + 1) * P].bitcast(FP8X4), rhs_scale=q1_scales[:, h * P : (h + 1) * P], start=False, stop=r == PACK - 1)
+                product(nc, scores[h][:, r, :], note_mx, block(r), q2_mx, block(h), start=r == 0, stop=False)
+        q_bf = sb.tile([P, Q, PACK], BF16, name="q_bf", align_bytes=ALIGN)
+        interleave(nc.vector.tensor_copy, q_bf[:], q_raw[:])
+        q_mx = quantize(nc, sb, "q", q_bf[:].rearrange("p w t -> p (w t)"))
+
+        me_listed = sb.tile([P, PACK, Q], F32, name="me_listed")
+        for j in range(PACK):
+            gather_scalar(me_listed[:, j, :], me[j], idx3[:])
+
+        val_listed = [sb.tile([P, I], BF16, name="val_listed%d" % j, align_bytes=ALIGN) for j in range(PACK)]
+        gather_vector(val_listed[0][:], val_pool[0], idx[:])
+
+        w_bf = sb.tile([P, Q, PACK], BF16, name="w_bf", tag="val_pool0", align_bytes=ALIGN)
+        for h in range(2):
+            for r in range(PACK):
+                product(
+                    nc, scores[h][:, r, :], (key_words, key_scales), block(r), q_mx, block(h),
+                    start=False, stop=r == PACK - 1, s_dtype=FP4X4,
+                )
             gate = sb.tile([P, P, PACK], F32, name="gate%d" % h)
             nc.scalar.activation(gate[:], scores[h][:].rearrange("p r q -> p q r"), SIGMOID)
-            nc.vector.tensor_tensor(out=w_bf[:, h * P : (h + 1) * P, :], in0=gate[:], in1=os_sb[:].unsqueeze(1).to_broadcast([P, P, PACK]), op=MULT)
-        w_codes, w_scales = quantize(nc, sb, "w", w_bf[:].rearrange("p q r -> p (q r)"), Q)
-        acc = ps.tile([P, BANK], F32, name="me_acc", tag="bank6")
-        nc.tensor.matmul_mx(out=acc[:], lhsT=wm_codes[:, 0:128].bitcast(FP8X4), lhsT_scale=wm_scales[:, 0:128], rhs=ms1_codes[:, 0:BANK].bitcast(FP8X4), rhs_scale=ms1_scales[:, 0:BANK], start=True, stop=True)
-        nc.scalar.copy(out=me[0][:, 1 * BANK : 2 * BANK], in_=acc[:])
-        acc = ps.tile([P, BANK], F32, name="me_acc", tag="bank7")
-        nc.tensor.matmul_mx(out=acc[:], lhsT=wm_codes[:, 128:256].bitcast(FP8X4), lhsT_scale=wm_scales[:, 128:256], rhs=ms1_codes[:, 0:BANK].bitcast(FP8X4), rhs_scale=ms1_scales[:, 0:BANK], start=True, stop=True)
-        nc.scalar.copy(out=me[1][:, 1 * BANK : 2 * BANK], in_=acc[:])
-        acc = ps.tile([P, BANK], F32, name="me_acc", tag="bank0")
-        nc.tensor.matmul_mx(out=acc[:], lhsT=wm_codes[:, 256:384].bitcast(FP8X4), lhsT_scale=wm_scales[:, 256:384], rhs=ms1_codes[:, 0:BANK].bitcast(FP8X4), rhs_scale=ms1_scales[:, 0:BANK], start=True, stop=True)
-        nc.scalar.copy(out=me[2][:, 1 * BANK : 2 * BANK], in_=acc[:])
-        acc = ps.tile([P, BANK], F32, name="me_acc", tag="bank1")
-        nc.tensor.matmul_mx(out=acc[:], lhsT=wm_codes[:, 384:512].bitcast(FP8X4), lhsT_scale=wm_scales[:, 384:512], rhs=ms1_codes[:, 0:BANK].bitcast(FP8X4), rhs_scale=ms1_scales[:, 0:BANK], start=True, stop=True)
-        nc.scalar.copy(out=me[3][:, 1 * BANK : 2 * BANK], in_=acc[:])
-        nc.vector.tensor_copy(out=me_listed[:, 0, :], in_=me[0][:].indirect(idx3[:]))
-        nc.scalar.activation(me_listed[:, 1, :], me[1][:].indirect(idx3[:]), COPY)
-        nc.scalar.activation(me_listed[:, 2, :], me[2][:].indirect(idx3[:]), COPY)
-        nc.scalar.activation(me_listed[:, 3, :], me[3][:].indirect(idx3[:]), COPY)
-        listed = sb.tile([P, I], BF16, name="val_listed0", align_bytes=64)
-        nc.vector.tensor_copy(out=listed[:], in_=val_pool0[:].indirect(idx[:]))
-        pairs = listed[:].bitcast(F32)
-        turned = ps.tile([P, 2, P], F32, name="turned", tag="bank4")
-        for u in range(2):
-            nc.tensor.transpose(turned[:, u, :], pairs[:, u::2], ident[:])
-        val_bf = sb.tile([P, P, PACK], BF16, name="val_bf0", align_bytes=64)
-        nc.vector.tensor_copy(out=val_bf[:].bitcast(F32), in_=turned[:].rearrange("p u e -> p e u"))
-        val0_codes, val0_scales = quantize(nc, sb, "val0", val_bf[:].rearrange("p e r -> p (e r)"), P)
-        listed = sb.tile([P, I], BF16, name="val_listed1", align_bytes=64)
-        nc.scalar.activation(listed[:], val_pool1[:].indirect(idx[:]), COPY)
-        pairs = listed[:].bitcast(F32)
-        turned = ps.tile([P, 2, P], F32, name="turned", tag="bank5")
-        for u in range(2):
-            nc.tensor.transpose(turned[:, u, :], pairs[:, u::2], ident[:])
-        val_bf = sb.tile([P, P, PACK], BF16, name="val_bf1", align_bytes=64)
-        nc.vector.tensor_copy(out=val_bf[:].bitcast(F32), in_=turned[:].rearrange("p u e -> p e u"))
-        val1_codes, val1_scales = quantize(nc, sb, "val1", val_bf[:].rearrange("p e r -> p (e r)"), P)
-        listed = sb.tile([P, I], BF16, name="val_listed2", align_bytes=64)
-        nc.scalar.activation(listed[:], val_pool2[:].indirect(idx[:]), COPY)
-        pairs = listed[:].bitcast(F32)
-        turned = ps.tile([P, 2, P], F32, name="turned", tag="bank6")
-        for u in range(2):
-            nc.tensor.transpose(turned[:, u, :], pairs[:, u::2], ident[:])
-        val_bf = sb.tile([P, P, PACK], BF16, name="val_bf2", align_bytes=64)
-        nc.vector.tensor_copy(out=val_bf[:].bitcast(F32), in_=turned[:].rearrange("p u e -> p e u"))
-        val2_codes, val2_scales = quantize(nc, sb, "val2", val_bf[:].rearrange("p e r -> p (e r)"), P)
-        listed = sb.tile([P, I], BF16, name="val_listed3", align_bytes=64)
-        nc.scalar.activation(listed[:], val_pool3[:].indirect(idx[:]), COPY)
-        pairs = listed[:].bitcast(F32)
-        turned = ps.tile([P, 2, P], F32, name="turned", tag="bank7")
-        for u in range(2):
-            nc.tensor.transpose(turned[:, u, :], pairs[:, u::2], ident[:])
-        val_bf = sb.tile([P, P, PACK], BF16, name="val_bf3", align_bytes=64)
-        nc.scalar.copy(out=val_bf[:].bitcast(F32), in_=turned[:].rearrange("p u e -> p e u"))
-        val3_codes, val3_scales = quantize(nc, sb, "val3", val_bf[:].rearrange("p e r -> p (e r)"), P)
-        o01 = ps.tile([P, 2, Q], F32, name="o01", tag="bank6")
-        nc.tensor.matmul_mx(out=o01[:, 0, :], lhsT=val0_codes[:, 0:P].bitcast(FP8X4), lhsT_scale=val0_scales[:, 0:P], rhs=w_codes[:, 0:Q].bitcast(FP8X4), rhs_scale=w_scales[:, 0:Q], start=True, stop=True)
-        nc.tensor.matmul_mx(out=o01[:, 1, :], lhsT=val1_codes[:, 0:P].bitcast(FP8X4), lhsT_scale=val1_scales[:, 0:P], rhs=w_codes[:, 0:Q].bitcast(FP8X4), rhs_scale=w_scales[:, 0:Q], start=True, stop=True)
-        nc.vector.tensor_tensor(out=y[:, 0:2, :], in0=o01[:], in1=me_listed[:, 0:2, :], op=MULT)
-        nc.sync.dma_start(out=out_rows[:, 0:2, :], in_=y[:, 0:2, :])
-        o = ps.tile([P, Q], F32, name="o", tag="bank4")
-        nc.tensor.matmul_mx(out=o[:], lhsT=val2_codes[:, 0:P].bitcast(FP8X4), lhsT_scale=val2_scales[:, 0:P], rhs=w_codes[:, 0:Q].bitcast(FP8X4), rhs_scale=w_scales[:, 0:Q], start=True, stop=True)
-        nc.vector.tensor_tensor(out=y[:, 2, :], in0=o[:], in1=me_listed[:, 2, :], op=MULT)
-        nc.sync.dma_start(out=out_rows[:, 2, :], in_=y[:, 2, :])
-        o = ps.tile([P, Q], F32, name="o", tag="bank0")
-        nc.tensor.matmul_mx(out=o[:], lhsT=val3_codes[:, 0:P].bitcast(FP8X4), lhsT_scale=val3_scales[:, 0:P], rhs=w_codes[:, 0:Q].bitcast(FP8X4), rhs_scale=w_scales[:, 0:Q], start=True, stop=True)
-        nc.vector.tensor_tensor(out=y[:, 3, :], in0=o[:], in1=me_listed[:, 3, :], op=MULT)
-        nc.sync.dma_start(out=out_rows[:, 3, :], in_=y[:, 3, :])
-        y_bf = sb.tile([P, Q, PACK], BF16, name="y_bf", align_bytes=64)
-        interleave(nc, y_bf[:], y[:])
-        y_codes, y_scales = quantize(nc, sb, "y", y_bf[:].rearrange("p q j -> p (q j)"), Q)
+            nc.vector.tensor_tensor(
+                out=w_bf[:, block(h), :], in0=gate[:], in1=os_sb[:].unsqueeze(1).to_broadcast([P, P, PACK]), op=MULT
+            )
+        w_mx = quantize(nc, sb, "w", w_bf[:].rearrange("p q r -> p (q r)"))
+
+        out_rows = out_0.rearrange("(p j) q -> p j q", j=PACK)
+
+        def turn(j):
+            pairs = val_listed[j][:].bitcast(F32)
+            turned = bank_tile("turned", [P, 2, P], 2 + j)
+            for u in range(2):
+                nc.tensor.transpose(turned[:, u, :], pairs[:, u::2], ident[:])
+            return turned
+
+        def leave_bank(j, turned, copy, pool=sb, offset=None):
+            val_bf = pool.tile([P, P, PACK], BF16, name="val_bf%d" % j, align_bytes=ALIGN, offset=offset)
+            copy(out=val_bf[:].bitcast(F32), in_=turned[:].rearrange("p u e -> p e u"))
+            return val_bf
+
+        def quantize_values(j, val_bf):
+            return quantize(nc, sb, "val%d" % j, val_bf[:].rearrange("p e r -> p (e r)"))
+
+        def weigh(j, val_mx):
+            o = bank_tile("o", [P, Q], 3 + j)
+            product(nc, o[:], val_mx, block(0), w_mx, block(0, Q))
+            nc.vector.tensor_tensor(out=y[:, j, :], in0=o[:], in1=me_listed[:, j, :], op=MULT)
+            nc.sync.dma_start(out=out_rows[:, j, :], in_=y[:, j, :])
+
+        val0_mx = quantize_values(0, leave_bank(0, turn(0), nc.vector.tensor_copy))
+        gather_scalar(val_listed[1][:], val_pool[1], idx[:])
+        val1_mx = quantize_values(1, leave_bank(1, turn(1), nc.vector.tensor_copy))
+        gather_scalar(val_listed[2][:], val_pool[2], idx[:])
+        turned2 = turn(2)
+        gather_vector(val_listed[3][:, : I // 2], val_pool[3], idx[:, : LIST_COLS // 2])
+        gather_scalar(val_listed[3][:, I // 2 :], val_pool[3], idx[:, LIST_COLS // 2 :])
+        y = reused.tile([P, PACK, Q], F32, name="y", align_bytes=ALIGN, offset=0)
+        val2_bf = leave_bank(2, turned2, nc.vector.tensor_copy, reused, 4 * PACK * Q)
+        weigh(0, val0_mx)
+        val2_mx = quantize_values(2, val2_bf)
+        weigh(1, val1_mx)
+        val3_mx = quantize_values(3, leave_bank(3, turn(3), nc.scalar.copy))
+        weigh(2, val2_mx)
+        weigh(3, val3_mx)
+
+        y_bf = sb.tile([P, Q, PACK], BF16, name="y_bf", align_bytes=ALIGN)
+        interleave(nc.vector.tensor_copy, y_bf[:, :Y_VECTOR_COLS, :], y[:, :, :Y_VECTOR_COLS])
+        interleave(nc.scalar.copy, y_bf[:, Y_VECTOR_COLS:, :], y[:, :, Y_VECTOR_COLS:])
+        y_codes, y_scales = quantize(nc, sb, "y", y_bf[:].rearrange("p q j -> p (q j)"))
         nc.sync.dma_start(out=out_1[0].rearrange("p q j -> p (q j)").bitcast(I32), in_=y_codes[:].bitcast(I32))
         for quad in range(4):
             queue = nc.scalar if quad % 2 == 0 else nc.sync
-            queue.dma_start(out=out_2[0, 4 * quad : 4 * quad + 4, :].bitcast(I32), in_=y_scales[32 * quad : 32 * quad + 4, :].bitcast(I32))
+            queue.dma_start(
+                out=out_2[0, 4 * quad : 4 * quad + 4, :].bitcast(I32),
+                in_=y_scales[32 * quad : 32 * quad + 4, :].bitcast(I32),
+            )

@@ -23,7 +23,9 @@ PACK = 4
 BANK = 512
 ALIGN = 64
 LIST_COLS = I // 16
-Y_VECTOR_COLS = 160
+Y_SCALAR_COLS = 96
+O_BANKS = (3, 7, 5)
+LAST_BANKS = (6, 0)
 
 
 def interleave(copy, dst, src):
@@ -106,6 +108,9 @@ def tile_attend_twosources_remembered_lean_pl_kernel(
         key_scale_pool = sb.tile([P, T], U8, name="key_scale_pool", align_bytes=ALIGN)
         nc.vector.memset(key_scale_pool[:].bitcast(I32), 0)
 
+        os_sb = sb.tile([P, PACK], F32, name="os_sb")
+        nc.gpsimd.dma_start(out=os_sb[:], in_=slot_factor.rearrange("o (p r) -> (o p) r", r=PACK))
+
         key_word_pool = sb.tile([P, T], U16, name="key_word_pool", align_bytes=ALIGN)
         nc.sync.dma_start(out=key_word_pool[:].bitcast(I32), in_=keys_words[0].bitcast(I32))
         idx = load_list("idx", offs)
@@ -114,10 +119,10 @@ def tile_attend_twosources_remembered_lean_pl_kernel(
         note_pool = [load_plane("note_pool0", notes, 0)]
         ms_raw = [load_rows("ms_raw0", mstore[:, block(0, BANK)])]
         note_pool.append(load_plane("note_pool1", notes, 1))
-        for quad in range(4):
+        for row in range(4):
             nc.sync.dma_start(
-                out=key_scale_pool[32 * quad : 32 * quad + 4, :].bitcast(I32),
-                in_=keys_scales[0, 4 * quad : 4 * quad + 4, :].bitcast(I32),
+                out=key_scale_pool[row:P:32, :].bitcast(I32),
+                in_=keys_scales[0, row:16:4, :].bitcast(I32),
             )
         ms_raw.append(load_rows("ms_raw1", mstore[:, block(1, BANK)]))
         note_pool.append(load_plane("note_pool2", notes, 2))
@@ -125,8 +130,6 @@ def tile_attend_twosources_remembered_lean_pl_kernel(
         idx3 = load_list("idx3", offs3)
         q2_raw = load_rows("q2_raw", query2)
         q_raw = load_rows("q_raw", query)
-        os_sb = sb.tile([P, PACK], F32, name="os_sb")
-        nc.sync.dma_start(out=os_sb[:], in_=slot_factor.rearrange("o (p r) -> (o p) r", r=PACK))
         val_pool = [load_plane("val_pool%d" % j, vals, j) for j in range(PACK - 1)]
         val_pool.append(load_plane("val_pool3", vals, 3, reused, 0))
 
@@ -221,7 +224,7 @@ def tile_attend_twosources_remembered_lean_pl_kernel(
             return quantize(nc, sb, "val%d" % j, val_bf[:].rearrange("p e r -> p (e r)"))
 
         def weigh(j, val_mx):
-            o = bank_tile("o", [P, Q], 3 + j)
+            o = bank_tile("o", [P, Q], O_BANKS[j])
             product(nc, o[:], val_mx, block(0), w_mx, block(0, Q))
             nc.vector.tensor_tensor(out=y[:, j, :], in0=o[:], in1=me_listed[:, j, :], op=MULT)
             nc.sync.dma_start(out=out_rows[:, j, :], in_=y[:, j, :])
@@ -234,18 +237,30 @@ def tile_attend_twosources_remembered_lean_pl_kernel(
         gather_vector(val_listed[3][:, : I // 2], val_pool[3], idx[:, : LIST_COLS // 2])
         gather_scalar(val_listed[3][:, I // 2 :], val_pool[3], idx[:, LIST_COLS // 2 :])
         y = reused.tile([P, PACK, Q], F32, name="y", align_bytes=ALIGN, offset=0)
-        val2_bf = leave_bank(2, turned2, nc.vector.tensor_copy, reused, 4 * PACK * Q)
+        val2_bf = leave_bank(2, turned2, nc.scalar.copy, reused, 4 * PACK * Q)
         weigh(0, val0_mx)
-        val2_mx = quantize_values(2, val2_bf)
         weigh(1, val1_mx)
+        val2_mx = quantize_values(2, val2_bf)
         val3_mx = quantize_values(3, leave_bank(3, turn(3), nc.scalar.copy))
         weigh(2, val2_mx)
-        weigh(3, val3_mx)
+        for h in range(2):
+            o = bank_tile("o", [P, P], LAST_BANKS[h])
+            product(nc, o[:], val3_mx, block(0), w_mx, block(h))
+            nc.vector.tensor_tensor(out=y[:, 3, block(h)], in0=o[:], in1=me_listed[:, 3, block(h)], op=MULT)
+        nc.sync.dma_start(out=out_rows[:, 3, :], in_=y[:, 3, :])
 
         y_bf = sb.tile([P, Q, PACK], BF16, name="y_bf", align_bytes=ALIGN)
-        interleave(nc.vector.tensor_copy, y_bf[:, :Y_VECTOR_COLS, :], y[:, :, :Y_VECTOR_COLS])
-        interleave(nc.scalar.copy, y_bf[:, Y_VECTOR_COLS:, :], y[:, :, Y_VECTOR_COLS:])
-        y_codes, y_scales = quantize(nc, sb, "y", y_bf[:].rearrange("p q j -> p (q j)"))
+        interleave(nc.scalar.copy, y_bf[:, :Y_SCALAR_COLS, :], y[:, :, :Y_SCALAR_COLS])
+        interleave(nc.vector.tensor_copy, y_bf[:, Y_SCALAR_COLS:P, :], y[:, :, Y_SCALAR_COLS:P])
+        interleave(nc.vector.tensor_copy, y_bf[:, P:, :], y[:, :, P:])
+        y_codes = sb.tile([P, Q], U32, name="y_codes", align_bytes=ALIGN)
+        y_scales = sb.tile([P, Q], U8, name="y_scales", align_bytes=ALIGN)
+        for h in range(2):
+            nc.vector.quantize_mx(
+                out=y_codes[:, block(h)].bitcast(FP8X4),
+                scales=y_scales[:, block(h)],
+                in_=y_bf[:, block(h), :].rearrange("p q j -> p (q j)"),
+            )
         nc.sync.dma_start(out=out_1[0].rearrange("p q j -> p (q j)").bitcast(I32), in_=y_codes[:].bitcast(I32))
         for quad in range(4):
             queue = nc.scalar if quad % 2 == 0 else nc.sync

from contextlib import ExitStack

import concourse.mybir as mybir
from concourse.masks import make_identity

D, T, I, Q, E, U, M, C = 512, 2048, 512, 256, 512, 1024, 1024, 512
FLOPS = 2 * (2 * D * Q * I + I * E * Q + C * E * M)

F32 = mybir.dt.float32
BF16 = mybir.dt.bfloat16
I32 = mybir.dt.int32
U32 = mybir.dt.uint32
U16 = mybir.dt.uint16
U8 = mybir.dt.uint8
FP8X4 = mybir.dt.float8_e4m3fn_x4
FP4X4 = mybir.dt.float4_e2m1fn_x4
COPY = mybir.ActivationFunctionType.Copy
SIGMOID = mybir.ActivationFunctionType.Sigmoid
MULT = mybir.AluOpType.mult

P = 128
PACK = 4
BANK = 512
ALIGN = 64
LIST_COLS = I // 16
Y_SCALAR_COLS = 96
O_BANKS = (3, 7, 5)
LAST_BANKS = (6, 0)


def interleave(copy, dst, src):
    copy(
        out=dst.rearrange("p (c i) t -> p c t i", i=PACK),
        in_=src.rearrange("p t (c i) -> p c t i", i=PACK),
    )


def deal_and_interleave(nc, dst, src):
    nc.vector.tensor_copy(
        out=dst.rearrange("p r s t -> p s t r"),
        in_=src.rearrange("p t (s r) -> p s t r", r=PACK),
    )


def quantize(nc, pool, name, grouped):
    width = grouped.shape[1] // PACK
    codes = pool.tile([P, width], U32, name=name + "_codes", align_bytes=ALIGN)
    scales = pool.tile([P, width], U8, name=name + "_scales", align_bytes=ALIGN)
    nc.vector.quantize_mx(out=codes[:].bitcast(FP8X4), scales=scales[:], in_=grouped)
    return codes, scales


def product(nc, out, stationary, s_cols, moving, m_cols, start=True, stop=True, s_dtype=FP8X4):
    nc.tensor.matmul_mx(
        out=out,
        lhsT=stationary[0][:, s_cols].bitcast(s_dtype),
        lhsT_scale=stationary[1][:, s_cols],
        rhs=moving[0][:, m_cols].bitcast(FP8X4),
        rhs_scale=moving[1][:, m_cols],
        start=start,
        stop=stop,
    )


def block(k, width=P):
    return slice(k * width, (k + 1) * width)


def tile_attend_twosources_remembered_lean_pl_kernel(
    tc, query, query2, keys_words, keys_scales, notes, slot_factor, vals, wm, mstore, offs, offs2, offs3, out_0, out_1, out_2
):
    nc = tc.nc
    with ExitStack() as ctx:
        lists = ctx.enter_context(tc.tile_pool(name="lists", bufs=1))
        sb = ctx.enter_context(tc.tile_pool(name="sb", bufs=1))
        reused = ctx.enter_context(tc.tile_pool(name="reused", bufs=1))
        ps = ctx.enter_context(tc.psum_pool(name="ps", bufs=1))

        def bank_tile(name, shape, bank):
            return ps.tile(shape, F32, name=name, tag="bank%d" % bank)

        def load_rows(name, src):
            rows = sb.tile([P, PACK, src.shape[1]], F32, name=name)
            nc.sync.dma_start(out=rows[:], in_=src.rearrange("(p t) w -> p t w", t=PACK))
            return rows

        def load_plane(name, src, t, pool=sb, offset=None):
            plane = pool.tile([P, src.shape[1]], F32, name=name, align_bytes=ALIGN, offset=offset)
            nc.sync.dma_start(out=plane[:], in_=src.rearrange("(p t) w -> p t w", t=PACK)[:, t, :])
            return plane

        def load_list(name, src):
            offsets = lists.tile([P, src.shape[1]], U16, name=name)
            nc.sync.dma_start(offsets[:], src)
            return offsets

        def gather_vector(out, window, offsets):
            nc.vector.tensor_copy(out=out, in_=window[:].indirect(offsets))

        def gather_scalar(out, window, offsets):
            nc.scalar.activation(out, window[:].indirect(offsets), COPY)

        warm_in = sb.tile([P, 1], F32, name="warm_in")
        nc.vector.memset(warm_in[:], 0.0)
        warm_out = sb.tile([P, 1], F32, name="warm_out")
        nc.scalar.activation(warm_out[:], warm_in[:], SIGMOID)

        key_scale_pool = sb.tile([P, T], U8, name="key_scale_pool", align_bytes=ALIGN)
        nc.vector.memset(key_scale_pool[:].bitcast(I32), 0)

        os_sb = sb.tile([P, PACK], F32, name="os_sb")
        nc.gpsimd.dma_start(out=os_sb[:], in_=slot_factor.rearrange("o (p r) -> (o p) r", r=PACK))

        key_word_pool = sb.tile([P, T], U16, name="key_word_pool", align_bytes=ALIGN)
        nc.sync.dma_start(out=key_word_pool[:].bitcast(I32), in_=keys_words[0].bitcast(I32))
        idx = load_list("idx", offs)
        wm_raw = load_rows("wm_raw", wm)
        idx2 = load_list("idx2", offs2)
        note_pool = [load_plane("note_pool0", notes, 0)]
        ms_raw = [load_rows("ms_raw0", mstore[:, block(0, BANK)])]
        note_pool.append(load_plane("note_pool1", notes, 1))
        for row in range(4):
            nc.sync.dma_start(
                out=key_scale_pool[row:P:32, :].bitcast(I32),
                in_=keys_scales[0, row:16:4, :].bitcast(I32),
            )
        ms_raw.append(load_rows("ms_raw1", mstore[:, block(1, BANK)]))
        note_pool.append(load_plane("note_pool2", notes, 2))
        note_pool.append(load_plane("note_pool3", notes, 3))
        idx3 = load_list("idx3", offs3)
        q2_raw = load_rows("q2_raw", query2)
        q_raw = load_rows("q_raw", query)
        val_pool = [load_plane("val_pool%d" % j, vals, j) for j in range(PACK - 1)]
        val_pool.append(load_plane("val_pool3", vals, 3, reused, 0))

        ident = sb.tile([P, P], F32, name="ident")
        make_identity(nc, ident[:])

        me = [sb.tile([P, M], F32, name="me%d" % j) for j in range(PACK)]
        note_listed = sb.tile([P, PACK, I], BF16, name="note_listed", align_bytes=ALIGN)

        key_listed = sb.tile([P, I], U16, name="key_listed", align_bytes=ALIGN)
        gather_vector(key_listed[:], key_word_pool, idx[:])
        key_words = sb.tile([P, I], U16, name="key_words", align_bytes=ALIGN)
        nc.vector.tensor_copy(
            out=key_words[:].rearrange("p (r s) -> p r s", r=PACK), in_=key_listed[:].rearrange("p (s r) -> p r s", r=PACK)
        )

        wm_bf = sb.tile([P, PACK, P, PACK], BF16, name="wm_bf", align_bytes=ALIGN)
        deal_and_interleave(nc, wm_bf[:], wm_raw[:])
        wm_mx = quantize(nc, sb, "wm", wm_bf[:].rearrange("p r s t -> p (r s t)"))

        def quantize_store_half(h):
            ms_bf = sb.tile([P, BANK, PACK], BF16, name="ms_bf%d" % h, align_bytes=ALIGN)
            interleave(nc.vector.tensor_copy, ms_bf[:], ms_raw[h][:])
            return quantize(nc, sb, "ms%d" % h, ms_bf[:].rearrange("p w t -> p (w t)"))

        def make_memories(h, ms_mx):
            for j in range(PACK):
                acc = bank_tile("me_acc", [P, BANK], PACK * h + j)
                product(nc, acc[:], wm_mx, block(j), ms_mx, block(0, BANK))
                nc.scalar.copy(out=me[j][:, block(h, BANK)], in_=acc[:])

        gather_scalar(note_listed[:, 0, :], note_pool[0], idx2[:])
        make_memories(0, quantize_store_half(0))
        gather_scalar(note_listed[:, 1, :], note_pool[1], idx2[:])
        key_scales = sb.tile([P, I], U8, name="key_scales", align_bytes=ALIGN)
        gather_vector(key_scales[:].rearrange("p (r s) -> p s r", r=PACK), key_scale_pool, idx[:])
        ms1_mx = quantize_store_half(1)
        gather_scalar(note_listed[:, 2, :], note_pool[2], idx2[:])
        make_memories(1, ms1_mx)
        gather_vector(note_listed[:, 3, :], note_pool[3], idx2[:])

        note_bf = sb.tile([P, PACK, P, PACK], BF16, name="note_bf", align_bytes=ALIGN)
        deal_and_interleave(nc, note_bf[:], note_listed[:])
        q2_bf = sb.tile([P, Q, PACK], BF16, name="q2_bf", align_bytes=ALIGN)
        interleave(nc.vector.tensor_copy, q2_bf[:], q2_raw[:])
        note_mx = quantize(nc, sb, "note", note_bf[:].rearrange("p r s t -> p (r s t)"))
        q2_mx = quantize(nc, sb, "q2", q2_bf[:].rearrange("p w t -> p (w t)"))
        scores = [bank_tile("scores%d" % h, [P, PACK, P], h) for h in range(2)]
        for h in range(2):
            for r in range(PACK):
                product(nc, scores[h][:, r, :], note_mx, block(r), q2_mx, block(h), start=r == 0, stop=False)
        q_bf = sb.tile([P, Q, PACK], BF16, name="q_bf", align_bytes=ALIGN)
        interleave(nc.vector.tensor_copy, q_bf[:], q_raw[:])
        q_mx = quantize(nc, sb, "q", q_bf[:].rearrange("p w t -> p (w t)"))

        me_listed = sb.tile([P, PACK, Q], F32, name="me_listed")
        for j in range(PACK):
            gather_scalar(me_listed[:, j, :], me[j], idx3[:])

        val_listed = [sb.tile([P, I], BF16, name="val_listed%d" % j, align_bytes=ALIGN) for j in range(PACK)]
        gather_vector(val_listed[0][:], val_pool[0], idx[:])

        w_bf = sb.tile([P, Q, PACK], BF16, name="w_bf", tag="val_pool0", align_bytes=ALIGN)
        for h in range(2):
            for r in range(PACK):
                product(
                    nc, scores[h][:, r, :], (key_words, key_scales), block(r), q_mx, block(h),
                    start=False, stop=r == PACK - 1, s_dtype=FP4X4,
                )
            gate = sb.tile([P, P, PACK], F32, name="gate%d" % h)
            nc.scalar.activation(gate[:], scores[h][:].rearrange("p r q -> p q r"), SIGMOID)
            nc.vector.tensor_tensor(
                out=w_bf[:, block(h), :], in0=gate[:], in1=os_sb[:].unsqueeze(1).to_broadcast([P, P, PACK]), op=MULT
            )
        w_mx = quantize(nc, sb, "w", w_bf[:].rearrange("p q r -> p (q r)"))

        out_rows = out_0.rearrange("(p j) q -> p j q", j=PACK)

        def turn(j):
            pairs = val_listed[j][:].bitcast(F32)
            turned = bank_tile("turned", [P, 2, P], 2 + j)
            for u in range(2):
                nc.tensor.transpose(turned[:, u, :], pairs[:, u::2], ident[:])
            return turned

        def leave_bank(j, turned, copy, pool=sb, offset=None):
            val_bf = pool.tile([P, P, PACK], BF16, name="val_bf%d" % j, align_bytes=ALIGN, offset=offset)
            copy(out=val_bf[:].bitcast(F32), in_=turned[:].rearrange("p u e -> p e u"))
            return val_bf

        def quantize_values(j, val_bf):
            return quantize(nc, sb, "val%d" % j, val_bf[:].rearrange("p e r -> p (e r)"))

        def weigh(j, val_mx):
            o = bank_tile("o", [P, Q], O_BANKS[j])
            product(nc, o[:], val_mx, block(0), w_mx, block(0, Q))
            nc.vector.tensor_tensor(out=y[:, j, :], in0=o[:], in1=me_listed[:, j, :], op=MULT)
            nc.sync.dma_start(out=out_rows[:, j, :], in_=y[:, j, :])

        val0_mx = quantize_values(0, leave_bank(0, turn(0), nc.vector.tensor_copy))
        gather_scalar(val_listed[1][:], val_pool[1], idx[:])
        val1_mx = quantize_values(1, leave_bank(1, turn(1), nc.vector.tensor_copy))
        gather_scalar(val_listed[2][:], val_pool[2], idx[:])
        turned2 = turn(2)
        gather_vector(val_listed[3][:, : I // 2], val_pool[3], idx[:, : LIST_COLS // 2])
        gather_scalar(val_listed[3][:, I // 2 :], val_pool[3], idx[:, LIST_COLS // 2 :])
        y = reused.tile([P, PACK, Q], F32, name="y", align_bytes=ALIGN, offset=0)
        val2_bf = leave_bank(2, turned2, nc.scalar.copy, reused, 4 * PACK * Q)
        weigh(0, val0_mx)
        weigh(1, val1_mx)
        val2_mx = quantize_values(2, val2_bf)
        val3_mx = quantize_values(3, leave_bank(3, turn(3), nc.scalar.copy))
        weigh(2, val2_mx)
        for h in range(2):
            o = bank_tile("o", [P, P], LAST_BANKS[h])
            product(nc, o[:], val3_mx, block(0), w_mx, block(h))
            nc.vector.tensor_tensor(out=y[:, 3, block(h)], in0=o[:], in1=me_listed[:, 3, block(h)], op=MULT)
        nc.sync.dma_start(out=out_rows[:, 3, :], in_=y[:, 3, :])

        y_bf = sb.tile([P, Q, PACK], BF16, name="y_bf", align_bytes=ALIGN)
        interleave(nc.scalar.copy, y_bf[:, :Y_SCALAR_COLS, :], y[:, :, :Y_SCALAR_COLS])
        interleave(nc.vector.tensor_copy, y_bf[:, Y_SCALAR_COLS:P, :], y[:, :, Y_SCALAR_COLS:P])
        interleave(nc.vector.tensor_copy, y_bf[:, P:, :], y[:, :, P:])
        y_codes = sb.tile([P, Q], U32, name="y_codes", align_bytes=ALIGN)
        y_scales = sb.tile([P, Q], U8, name="y_scales", align_bytes=ALIGN)
        for h in range(2):
            nc.vector.quantize_mx(
                out=y_codes[:, block(h)].bitcast(FP8X4),
                scales=y_scales[:, block(h)],
                in_=y_bf[:, block(h), :].rearrange("p q j -> p (q j)"),
            )
        nc.sync.dma_start(out=out_1[0].rearrange("p q j -> p (q j)").bitcast(I32), in_=y_codes[:].bitcast(I32))
        for quad in range(4):
            queue = nc.scalar if quad % 2 == 0 else nc.sync
            queue.dma_start(
                out=out_2[0, 4 * quad : 4 * quad + 4, :].bitcast(I32),
                in_=y_scales[32 * quad : 32 * quad + 4, :].bitcast(I32),
            )
